import numpy as np
import ml_dtypes


def mxq(x, axis, fmt="e4m3"):
    dtype, down = {"e4m3": (ml_dtypes.float8_e4m3fn, 7), "e5m2": (ml_dtypes.float8_e5m2, 14)}[fmt]
    v = np.moveaxis(np.asarray(x, np.float32).astype(ml_dtypes.bfloat16).astype(np.float64), axis, -1)
    blocks = v.reshape(v.shape[:-1] + (-1, 32))
    amax = np.abs(blocks).max(-1, keepdims=True)
    byte = np.maximum(np.where(amax > 0, np.frexp(amax)[1] - 1 + 127, 0) - down, 1)
    scale = np.exp2(byte - 127.0)
    codes = (blocks / scale).astype(np.float32).astype(dtype).astype(np.float64)
    return np.moveaxis((codes * scale).reshape(v.shape), -1, axis)


WIDE = False


def mx_kscale(k):
    if not WIDE:
        return np.ones(k)
    levels = np.array([10, -10, 5, -5, 0])
    if k % 512:
        return np.exp2(np.random.permutation(np.resize(levels, k // 32))).repeat(32)
    a = np.empty((k // 512, 16))
    for p in range(k // 512):
        a[p, :8] = np.random.permutation(np.resize(levels, 8))
        for g in range(8):
            far = levels[np.abs(levels - a[p, g]) >= 10]
            a[p, g + 8] = far[np.random.randint(len(far))]
    return np.exp2(a.ravel()).repeat(32)


def f64(x):
    return np.asarray(x).astype(np.float64)


def striped(idx):
    return np.tile(idx.reshape(-1, 16).T, (8, 1)).astype(np.uint16)


def unstriped(offs):
    return offs[:16].T.reshape(-1).astype(np.int64)


E2M1 = np.array([0.0, 0.5, 1.0, 1.5, 2.0, 3.0, 4.0, 6.0, -0.0, -0.5, -1.0, -1.5, -2.0, -3.0, -4.0, -6.0])


def pack_weight(w, fmt):
    k, n = w.shape
    w = f64(np.asarray(w, np.float32).astype(ml_dtypes.bfloat16)).reshape(k // 32, 32, n)
    amax = np.abs(w).max(1)
    if fmt == "e4m3":
        byte = np.frexp(amax)[1] - 1 + 127 - 7
    else:
        mant, ex = np.frexp(amax / 6.0)
        byte = np.where(mant > 0.5, ex, ex - 1) + 127
    byte = np.clip(np.where(amax > 0, byte, 1), 1, 254)
    scaled = (w * np.exp2(127.0 - byte)[:, None, :]).reshape(k, n).astype(np.float32)
    by_word = np.ascontiguousarray(scaled.reshape(k // 512, 128, 4, n).transpose(0, 1, 3, 2))
    if fmt == "e4m3":
        words = by_word.astype(ml_dtypes.float8_e4m3fn).view(np.uint8)
    else:
        c = by_word.astype(ml_dtypes.float4_e2m1fn).view(np.uint8) & 0xF
        words = (c[..., 0::2] | (c[..., 1::2] << 4)).reshape(k // 512, 128, 2 * n)
    return np.ascontiguousarray(words), np.ascontiguousarray(byte.astype(np.uint8).reshape(k // 512, 16, n))


def unpack_weight(words, scales, fmt):
    g, _, n = scales.shape
    words = np.ascontiguousarray(words).reshape(g, 128, n, -1)
    if fmt == "e4m3":
        vals = words.view(ml_dtypes.float8_e4m3fn).astype(np.float64)
    else:
        nib = np.empty((g, 128, n, 4), np.uint8)
        nib[..., 0::2] = words & 0xF
        nib[..., 1::2] = words >> 4
        vals = E2M1[nib]
    vals = vals * np.repeat(np.exp2(scales.astype(np.float64) - 127.0), 8, axis=1)[..., None]
    return vals.transpose(0, 1, 3, 2).reshape(g * 512, n)


def planes(y):
    n, m = y.shape
    v = y.astype(np.float32).astype(ml_dtypes.bfloat16).astype(np.float64).reshape(n // 32, 32, m)
    top = np.abs(v).max(1)
    byte = np.clip(np.where(top > 0, np.frexp(top)[1] - 1 + 127 - 7, 1), 1, 254)
    codes = (v * np.exp2(127.0 - byte)[:, None, :]).reshape(n, m).astype(np.float32).astype(ml_dtypes.float8_e4m3fn).view(np.uint8)
    words = codes.reshape(n // 512, 128, 4, m).transpose(0, 1, 3, 2)
    return np.ascontiguousarray(words), np.ascontiguousarray(byte.astype(np.uint8).reshape(n // 512, 16, m))


def relu2(v):
    return np.maximum(v, 0.0) ** 2


K, T, E, C, H, N, HOT = 1536, 512, 8, 128, 512, 512, 3


def by_expert(wq, xq):
    return np.concatenate([wq[e].T @ xq[:, e * C:(e + 1) * C] for e in range(E)], axis=1)


def setup_inputs():
    n = np.random.standard_normal
    s = mx_kscale(K)
    u = mx_kscale(H)
    first = np.random.permutation(np.repeat(np.arange(E), T // E))
    second = (first + 1 + np.random.permutation(np.repeat(np.arange(E - 1), -(-T // (E - 1)))[:T])) % E
    while np.bincount(second, minlength=E).max() != T // E:
        load = np.bincount(second, minlength=E); hi, lo = int(load.argmax()), int(load.argmin())
        t = np.flatnonzero((second == hi) & (first != lo))[0]; second[t] = lo
    slot_token = np.empty(E * C, np.int64); pos = np.empty((2, T), np.int64); fill = np.zeros(E, np.int64)
    place = np.stack([np.random.permutation(C) for _ in range(E)])
    for r, deal in enumerate((first, second)):
        for t in np.random.permutation(T):
            e = deal[t]; j = e * C + place[e, fill[e]]; fill[e] += 1; slot_token[j] = t; pos[r, t] = j
    g = np.random.uniform(0.2, 0.8, T)
    x = pack_weight(n((K, T)) * s[:, None], "e4m3")
    w1h = [pack_weight(m, "e4m3") for m in n((HOT, K, H)) / np.sqrt(K) / s[None, :, None] * u]
    w2h = [pack_weight(m, "e4m3") for m in n((HOT, H, N)) / np.sqrt(H) / u[None, :, None] ** 2]
    w1c = [pack_weight(m, "e2m1") for m in n((E - HOT, K, H)) / np.sqrt(K) / s[None, :, None] * u]
    w2c = [pack_weight(m, "e2m1") for m in n((E - HOT, H, N)) / np.sqrt(H) / u[None, :, None] ** 2]
    return {
        "x_words": x[0],
        "x_scales": x[1],
        "w1h_words": np.stack([m[0] for m in w1h]),
        "w1h_scales": np.stack([m[1] for m in w1h]),
        "w2h_words": np.stack([m[0] for m in w2h]),
        "w2h_scales": np.stack([m[1] for m in w2h]),
        "w1c_words": np.stack([m[0] for m in w1c]),
        "w1c_scales": np.stack([m[1] for m in w1c]),
        "w2c_words": np.stack([m[0] for m in w2c]),
        "w2c_scales": np.stack([m[1] for m in w2c]),
        "gate": np.stack([np.tile(g, (128, 1)), np.tile(1.0 - g, (128, 1))]).astype(np.float32),
        "offs": striped(slot_token),
        "pos1": striped(pos[0]),
        "pos2": striped(pos[1]),
    }


def reference(x_words, x_scales, w1h_words, w1h_scales, w2h_words, w2h_scales, w1c_words, w1c_scales, w2c_words, w2c_scales, gate, offs, pos1, pos2):
    w1h = np.stack([unpack_weight(w1h_words[e], w1h_scales[e], "e4m3") for e in range(HOT)])
    w2h = np.stack([unpack_weight(w2h_words[e], w2h_scales[e], "e4m3") for e in range(HOT)])
    w1c = np.stack([unpack_weight(w1c_words[e], w1c_scales[e], "e2m1") for e in range(E - HOT)])
    w2c = np.stack([unpack_weight(w2c_words[e], w2c_scales[e], "e2m1") for e in range(E - HOT)])
    idx = unstriped(offs)
    xq = unpack_weight(x_words, x_scales, "e4m3")[:, idx]
    w1 = [*w1h, *w1c]
    w2 = [*w2h, *w2c]
    h = relu2(by_expert(w1, xq))
    y = by_expert(w2, mxq(h, 0, "e4m3"))
    out = sum(f64(gate[r, :1]) * y[:, unstriped(p)] for r, p in enumerate((pos1, pos2)))
    out_0 = out
    return (out_0,) + planes(out_0)

@@ -1,0 +1,268 @@
+from contextlib import ExitStack
+
+import concourse.mybir as mybir
+from concourse.masks import make_identity
+
+K, T, E, C, H, N, HOT = 1536, 512, 8, 128, 512, 512, 3
+COLD = E - HOT
+FLOPS = 2 * E * C * (K * H + H * N)
+
+F32 = mybir.dt.float32
+BF16 = mybir.dt.bfloat16
+I32 = mybir.dt.int32
+U32 = mybir.dt.uint32
+U16 = mybir.dt.uint16
+U8 = mybir.dt.uint8
+FP8X4 = mybir.dt.float8_e4m3fn_x4
+FP4X4 = mybir.dt.float4_e2m1fn_x4
+ACT = mybir.ActivationFunctionType
+ALU = mybir.AluOpType
+
+P = 128
+PASSES = K // 512
+SLOTS = E * C
+ORDER = (7, 6, 5, 4, 3, 2, 1, 0)
+GROUPS = {7: 1, 6: 2, 4: 2, 2: 2, 0: 1}
+AFTER = {7: 4, 6: 2, 5: 0}
+LATE = 2
+REGION = 4096
+WORDS = 3072
+CHUNKS = ((0, 384), (384, 128))
+
+
+def tile_moe_hot_mlp_relu2_kernel(
+    tc, x_words, x_scales, w1h_words, w1h_scales, w2h_words, w2h_scales,
+    w1c_words, w1c_scales, w2c_words, w2c_scales, gate, offs, pos1, pos2, out_0, out_1, out_2,
+):
+    nc = tc.nc
+    with ExitStack() as ctx:
+        lists = ctx.enter_context(tc.tile_pool(name="lists", bufs=1))
+        keep = ctx.enter_context(tc.tile_pool(name="keep", bufs=1))
+        ring = ctx.enter_context(tc.tile_pool(name="ring", bufs=3))
+        reuse = ctx.enter_context(tc.tile_pool(name="reuse", bufs=1))
+        psum = ctx.enter_context(tc.psum_pool(name="psum", bufs=1))
+
+        def plane_tile(name, planes, engine):
+            t = keep.tile([P, planes * 512], U8, name=name, align_bytes=64)
+            engine.memset(t[:].bitcast(I32), 0)
+            return t
+
+        def load_planes(t, src, queue=nc.sync):
+            rows = src.bitcast(I32)
+            view = t[:].bitcast(I32).rearrange("p (g n) -> p g n", n=128)
+            for r in range(4):
+                queue.dma_start(out=view[r:P:32], in_=rows[:, r:16:4, :].rearrange("g q n -> q g n"))
+
+        s1a = plane_tile("s1a", 3 * PASSES, nc.vector)
+        xs = plane_tile("xs", PASSES, nc.vector)
+        xp = plane_tile("xp", 1, nc.vector)
+        s2c = plane_tile("s2c", COLD, nc.vector)
+        s1b = plane_tile("s1b", 2 * PASSES, nc.vector)
+        s1h = plane_tile("s1h", HOT * PASSES, nc.vector)
+        s2h = plane_tile("s2h", HOT, nc.vector)
+        s1 = {7: (s1a, 2), 6: (s1a, 1), 5: (s1a, 0), 4: (s1b, 1), 3: (s1b, 0), 2: (s1h, 2), 1: (s1h, 1), 0: (s1h, 0)}
+        ident = keep.tile([P, P], F32, name="ident")
+
+        offs_t = lists.tile([P, SLOTS // 16], U16, name="offs_t")
+        pos_t = [lists.tile([P, T // 16], U16, name="pos%d_t" % r) for r in (1, 2)]
+        xw = keep.tile([P, PASSES * T], I32, name="xw", align_bytes=64)
+        w1 = {}
+        w2 = {}
+
+        def load_w1(e):
+            if e < HOT:
+                t = keep.tile([P, PASSES * H * 4], U8, name="w1_%d" % e, align_bytes=64)
+                src = w1h_words[e].rearrange("s p i d -> p s (i d)").bitcast(I32)
+            else:
+                t = keep.tile([P, PASSES * H * 2], U8, name="w1_%d" % e, align_bytes=64)
+                src = w1c_words[e - HOT].bitcast(I32).rearrange("s p w -> p s w")
+            nc.sync.dma_start(out=t[:].bitcast(I32).rearrange("p (s w) -> p s w", s=PASSES), in_=src)
+            w1[e] = t
+
+        def load_w2(first, count):
+            if first < HOT:
+                width = N * 4
+                src = w2h_words[first:first + count, 0].rearrange("e p n d -> p e (n d)").bitcast(I32)
+            else:
+                width = N * 2
+                src = w2c_words[first - HOT:first - HOT + count, 0].bitcast(I32).rearrange("e p w -> p e w")
+            t = keep.tile([P, count * width], U8, name="w2_%d" % first, align_bytes=64)
+            nc.sync.dma_start(out=t[:].bitcast(I32).rearrange("p (e w) -> p e w", e=count), in_=src)
+            for i in range(count):
+                w2[first + i] = t[:, i * width:(i + 1) * width]
+
+        nc.sync.dma_start(offs_t[:], offs)
+        nc.sync.dma_start(
+            out=xw[:].rearrange("p (s t) -> p s t", s=PASSES),
+            in_=x_words.rearrange("s p t d -> p s (t d)").bitcast(I32),
+        )
+        flat = "e s b i -> (e s) b i"
+        load_planes(s1a, w1c_scales[2:5].rearrange(flat), nc.gpsimd)
+        make_identity(nc, ident[:])
+        for q in range(4):
+            nc.gpsimd.dma_start(
+                out=xp[:].bitcast(I32)[32 * q:32 * q + 4 * PASSES, :],
+                in_=x_scales.bitcast(I32)[:, 4 * q:4 * q + 4, :],
+            )
+        load_planes(s1h, w1h_scales.rearrange(flat), nc.gpsimd)
+        load_planes(xs, x_scales, nc.scalar)
+        load_w1(7)
+        load_w1(6)
+        load_w1(5)
+        load_planes(s2c, w2c_scales.rearrange(flat))
+        load_w2(5, 3)
+        load_planes(s1b, w1c_scales[0:2].rearrange(flat))
+        load_w1(4)
+        load_w1(3)
+        load_w2(3, 2)
+        load_w1(2)
+        load_planes(s2h, w2h_scales.rearrange(flat))
+        load_w1(1)
+        load_w2(1, 2)
+        load_w1(0)
+        load_w2(0, 1)
+        nc.sync.dma_start(pos_t[0][:], pos1)
+        nc.sync.dma_start(pos_t[1][:], pos2)
+        gate_t = keep.tile([P, 2, T], F32, name="gate_t")
+        nc.sync.dma_start(out=gate_t[:], in_=gate.rearrange("r p t -> p r t"))
+
+        y = keep.tile([P, 4 * SLOTS], F32, name="y")
+        y3 = y[:].rearrange("p (j u) -> p j u", j=4)
+        st = {}
+
+        def gather(last):
+            count = GROUPS[last]
+            e0 = last - count + 1
+            n = count * C
+            base = last * REGION
+            gw = reuse.tile([P, PASSES * n], U32, name="gw%d" % last, align_bytes=64, offset=base + WORDS - PASSES * n * 4)
+            o = offs_t[:, e0 * 8:(last + 1) * 8]
+            if last == HOT - 1:
+                gp = reuse.tile([P, HOT * C], U8, name="gp", align_bytes=64, offset=base + WORDS)
+                nc.vector.tensor_copy(gp[:], xp[:].indirect(offs_t[:, 0:HOT * 8]))
+                st["gp"] = gp
+            if last >= HOT:
+                gs = reuse.tile([P, PASSES * n], U8, name="gs%d" % last, align_bytes=64, offset=base + WORDS)
+            for s in range(PASSES):
+                nc.vector.tensor_copy(gw[:, s * n:(s + 1) * n], xw[:].bitcast(U32)[:, s * T:(s + 1) * T].indirect(o))
+                if last >= HOT:
+                    nc.vector.tensor_copy(gs[:, s * n:(s + 1) * n], xs[:, s * T:(s + 1) * T].indirect(o))
+            for e in range(e0, last + 1):
+                cols = [slice(s * n + (e - e0) * C, s * n + (e - e0 + 1) * C) for s in range(PASSES)]
+                if last >= HOT:
+                    st["g", e] = [(gw[:, c], gs[:, c]) for c in cols]
+                else:
+                    st["g", e] = [(gw[:, c], st["gp"][4 * s:P, e * C:(e + 1) * C]) for s, c in enumerate(cols)]
+
+        def layer1(e):
+            a = psum.tile([P, H], F32, name="a", bufs=2)
+            hot = e < HOT
+            width = H * (4 if hot else 2)
+            planes = s1[e][0]
+            first = s1[e][1] * PASSES
+            for s in range(PASSES):
+                nc.tensor.matmul_mx(
+                    out=a[:],
+                    lhsT=st["g", e][s][0].bitcast(FP8X4),
+                    lhsT_scale=st["g", e][s][1],
+                    rhs=w1[e][:, s * width:(s + 1) * width].bitcast(FP8X4 if hot else FP4X4),
+                    rhs_scale=planes[:, (first + s) * H:(first + s + 1) * H],
+                    start=(s == 0), stop=(s == PASSES - 1),
+                )
+            r = ring.tile([P, 4, P], F32, name="r")
+            if e < LATE:
+                nc.vector.tensor_scalar_max(r[:], a[:].rearrange("p (m j) -> p j m", j=4), 0.0)
+            else:
+                nc.scalar.activation(r[:], a[:].rearrange("p (m j) -> p j m", j=4), ACT.Relu)
+            st["r", e] = r
+
+        def turn1(e):
+            r = st["r", e]
+            b = psum.tile([P, 4, P], F32, name="b", bufs=2)
+            for j in range(4):
+                nc.tensor.transpose(b[:, j, :], r[:, j, :], ident[:])
+            if e in AFTER:
+                hb = reuse.tile([P, C, 4], BF16, name="hb%d" % e, align_bytes=64, offset=AFTER[e] * REGION + WORDS - 512)
+            else:
+                hb = ring.tile([P, C, 4], BF16, name="hb", align_bytes=64)
+            nc.scalar.activation(hb[:], b[:].rearrange("p j u -> p u j"), ACT.Square)
+            hq = ring.tile([P, C], U32, name="hq", align_bytes=64)
+            hs = ring.tile([P, C], U8, name="hs", align_bytes=64)
+            nc.vector.quantize_mx(out=hq[:].bitcast(FP8X4), scales=hs[:], in_=hb[:].rearrange("p u j -> p (u j)"))
+            st["q", e] = (hq, hs)
+
+        def layer2(e):
+            hq, hs = st["q", e]
+            hot = e < HOT
+            planes = s2h if hot else s2c
+            first = e if hot else e - HOT
+            c = psum.tile([P, N], F32, name="c", bufs=2)
+            nc.tensor.matmul_mx(
+                out=c[:],
+                lhsT=hq[:].bitcast(FP8X4),
+                lhsT_scale=hs[:],
+                rhs=w2[e].bitcast(FP8X4 if hot else FP4X4),
+                rhs_scale=planes[:, first * N:(first + 1) * N],
+                start=True, stop=True,
+            )
+            yt = ring.tile([P, 4, P], F32, name="yt")
+            if e < LATE:
+                nc.vector.tensor_copy(yt[:], c[:].rearrange("p (m j) -> p j m", j=4))
+            else:
+                nc.scalar.copy(yt[:], c[:].rearrange("p (m j) -> p j m", j=4))
+            st["yt", e] = yt
+
+        def turn2(e):
+            yt = st["yt", e]
+            d = psum.tile([P, 4, P], F32, name="d", bufs=2)
+            for j in range(4):
+                nc.tensor.transpose(d[:, j, :], yt[:, j, :], ident[:])
+            nc.scalar.copy(y3[:, :, e * C:(e + 1) * C], d[:])
+
+        gather(7)
+        gather(6)
+        for step in range(1, E + 4):
+            for back, stage in ((4, turn2), (2, turn1), (3, layer2), (1, layer1)):
+                if 0 <= step - back < E:
+                    e = ORDER[step - back]
+                    stage(e)
+                    if stage is turn1 and e in AFTER:
+                        gather(AFTER[e])
+
+        codes = keep.tile([P, T], I32, name="codes", align_bytes=64)
+        oscale = keep.tile([P, T], U8, name="oscale", align_bytes=64)
+        out_rows = out_0.rearrange("(p j) t -> p j t", j=4)
+        out_words = out_1[0].rearrange("p t d -> p (t d)").bitcast(I32)
+        for n, (t0, w) in enumerate(CHUNKS):
+            g = [keep.tile([P, 4, w], F32, name="g%d_%d" % (r, n)) for r in range(2)]
+            o = keep.tile([P, 4, w], F32, name="o_%d" % n)
+            step = 1 if n == 0 else 2
+            for j0 in range(0, 4, step):
+                j1 = j0 + step
+                for r in range(2):
+                    for j in range(j0, j1):
+                        src = y[:, j * SLOTS:(j + 1) * SLOTS].indirect(pos_t[r][:, t0 // 16:(t0 + w) // 16])
+                        if n == 0 and r == 0 and j < 2:
+                            nc.vector.tensor_copy(g[r][:, j, :], src)
+                        else:
+                            nc.scalar.activation(g[r][:, j, :], src, ACT.Copy)
+                for r in range(2):
+                    nc.vector.tensor_tensor(
+                        g[r][:, j0:j1, :], g[r][:, j0:j1, :],
+                        gate_t[:, r:r + 1, t0:t0 + w].to_broadcast([P, j1 - j0, w]), ALU.mult,
+                    )
+                nc.vector.tensor_tensor(o[:, j0:j1, :], g[0][:, j0:j1, :], g[1][:, j0:j1, :], ALU.add)
+            nc.sync.dma_start(out=out_rows[:, :, t0:t0 + w], in_=o[:])
+            ob = keep.tile([P, w, 4], BF16, name="ob_%d" % n, align_bytes=64)
+            if n == 0:
+                nc.scalar.copy(ob[:], o[:].rearrange("p j t -> p t j"))
+            else:
+                nc.vector.tensor_copy(ob[:], o[:].rearrange("p j t -> p t j"))
+            nc.vector.quantize_mx(
+                out=codes[:, t0:t0 + w].bitcast(FP8X4), scales=oscale[:, t0:t0 + w],
+                in_=ob[:].rearrange("p t j -> p (t j)"),
+            )
+            nc.sync.dma_start(out=out_words[:, t0:t0 + w], in_=codes[:, t0:t0 + w])
+        for r in range(4):
+            queue = nc.sync if r % 2 == 0 else nc.scalar
+            queue.dma_start(out=out_2[0].bitcast(I32)[r:16:4, :], in_=oscale[:].bitcast(I32)[r:P:32, :])

@@ -21,12 +21,7 @@ ALU = mybir.AluOpType
 P = 128
 PASSES = K // 512
 SLOTS = E * C
-ORDER = (7, 6, 5, 4, 3, 2, 1, 0)
-GROUPS = {7: 1, 6: 2, 4: 2, 2: 2, 0: 1}
-AFTER = {7: 4, 6: 2, 5: 0}
-LATE = 2
-REGION = 4096
-WORDS = 3072
+GROUPS = ((0, 1), (1, 2), (3, 2), (5, 2), (7, 1))
 CHUNKS = ((0, 384), (384, 128))
 
 
@@ -38,8 +33,7 @@ def tile_moe_hot_mlp_relu2_kernel(
     with ExitStack() as ctx:
         lists = ctx.enter_context(tc.tile_pool(name="lists", bufs=1))
         keep = ctx.enter_context(tc.tile_pool(name="keep", bufs=1))
-        ring = ctx.enter_context(tc.tile_pool(name="ring", bufs=3))
-        reuse = ctx.enter_context(tc.tile_pool(name="reuse", bufs=1))
+        ring = ctx.enter_context(tc.tile_pool(name="ring", bufs=8))
         psum = ctx.enter_context(tc.psum_pool(name="psum", bufs=1))
 
         def plane_tile(name, planes, engine):
@@ -47,20 +41,18 @@ def tile_moe_hot_mlp_relu2_kernel(
             engine.memset(t[:].bitcast(I32), 0)
             return t
 
-        def load_planes(t, src, queue=nc.sync):
+        def load_planes(t, src, queues=(nc.sync,)):
             rows = src.bitcast(I32)
             view = t[:].bitcast(I32).rearrange("p (g n) -> p g n", n=128)
             for r in range(4):
-                queue.dma_start(out=view[r:P:32], in_=rows[:, r:16:4, :].rearrange("g q n -> q g n"))
+                queues[r % len(queues)].dma_start(out=view[r:P:32], in_=rows[:, r:16:4, :].rearrange("g q n -> q g n"))
 
-        s1a = plane_tile("s1a", 3 * PASSES, nc.vector)
-        xs = plane_tile("xs", PASSES, nc.vector)
-        xp = plane_tile("xp", 1, nc.vector)
-        s2c = plane_tile("s2c", COLD, nc.vector)
-        s1b = plane_tile("s1b", 2 * PASSES, nc.vector)
-        s1h = plane_tile("s1h", HOT * PASSES, nc.vector)
+        xp = plane_tile("xp", 1, nc.gpsimd)
+        s1h = plane_tile("s1h", HOT * PASSES, nc.gpsimd)
+        s1c = plane_tile("s1c", COLD * PASSES, nc.vector)
+        xs = plane_tile("xs", PASSES - 1, nc.vector)
         s2h = plane_tile("s2h", HOT, nc.vector)
-        s1 = {7: (s1a, 2), 6: (s1a, 1), 5: (s1a, 0), 4: (s1b, 1), 3: (s1b, 0), 2: (s1h, 2), 1: (s1h, 1), 0: (s1h, 0)}
+        s2c = plane_tile("s2c", COLD, nc.vector)
         ident = keep.tile([P, P], F32, name="ident")
 
         offs_t = lists.tile([P, SLOTS // 16], U16, name="offs_t")
@@ -69,15 +61,17 @@ def tile_moe_hot_mlp_relu2_kernel(
         w1 = {}
         w2 = {}
 
-        def load_w1(e):
-            if e < HOT:
-                t = keep.tile([P, PASSES * H * 4], U8, name="w1_%d" % e, align_bytes=64)
-                src = w1h_words[e].rearrange("s p i d -> p s (i d)").bitcast(I32)
+        def load_w1(first, count):
+            if first < HOT:
+                width = PASSES * H * 4
+                src = w1h_words[first:first + count].rearrange("e s p i d -> p (e s) (i d)").bitcast(I32)
             else:
-                t = keep.tile([P, PASSES * H * 2], U8, name="w1_%d" % e, align_bytes=64)
-                src = w1c_words[e - HOT].bitcast(I32).rearrange("s p w -> p s w")
-            nc.sync.dma_start(out=t[:].bitcast(I32).rearrange("p (s w) -> p s w", s=PASSES), in_=src)
-            w1[e] = t
+                width = PASSES * H * 2
+                src = w1c_words[first - HOT:first - HOT + count].bitcast(I32).rearrange("e s p w -> p (e s) w")
+            t = keep.tile([P, count * width], U8, name="w1_%d" % first, align_bytes=64)
+            nc.sync.dma_start(out=t[:].bitcast(I32).rearrange("p (g w) -> p g w", g=count * PASSES), in_=src)
+            for i in range(count):
+                w1[first + i] = t[:, i * width:(i + 1) * width]
 
         def load_w2(first, count):
             if first < HOT:
@@ -91,36 +85,31 @@ def tile_moe_hot_mlp_relu2_kernel(
             for i in range(count):
                 w2[first + i] = t[:, i * width:(i + 1) * width]
 
+        flat = "e s b i -> (e s) b i"
+        make_identity(nc, ident[:])
         nc.sync.dma_start(offs_t[:], offs)
         nc.sync.dma_start(
             out=xw[:].rearrange("p (s t) -> p s t", s=PASSES),
             in_=x_words.rearrange("s p t d -> p s (t d)").bitcast(I32),
         )
-        flat = "e s b i -> (e s) b i"
-        load_planes(s1a, w1c_scales[2:5].rearrange(flat), nc.gpsimd)
-        make_identity(nc, ident[:])
         for q in range(4):
-            nc.gpsimd.dma_start(
+            (nc.scalar,)[q % 1].dma_start(
                 out=xp[:].bitcast(I32)[32 * q:32 * q + 4 * PASSES, :],
                 in_=x_scales.bitcast(I32)[:, 4 * q:4 * q + 4, :],
             )
-        load_planes(s1h, w1h_scales.rearrange(flat), nc.gpsimd)
-        load_planes(xs, x_scales, nc.scalar)
-        load_w1(7)
-        load_w1(6)
-        load_w1(5)
-        load_planes(s2c, w2c_scales.rearrange(flat))
-        load_w2(5, 3)
-        load_planes(s1b, w1c_scales[0:2].rearrange(flat))
-        load_w1(4)
-        load_w1(3)
-        load_w2(3, 2)
-        load_w1(2)
-        load_planes(s2h, w2h_scales.rearrange(flat))
-        load_w1(1)
-        load_w2(1, 2)
-        load_w1(0)
-        load_w2(0, 1)
+        load_w1(0, 1)
+        load_planes(s1h, w1h_scales.rearrange(flat), (nc.scalar, nc.sync,))
+        load_planes(xs, x_scales[1:PASSES], (nc.sync,))
+        load_planes(s1c, w1c_scales.rearrange(flat), (nc.scalar,))
+        load_w1(1, 1)
+        load_w1(2, 1)
+        load_w1(3, 2)
+        load_w1(5, 2)
+        load_w1(7, 1)
+        load_w2(0, 3)
+        load_planes(s2h, w2h_scales.rearrange(flat), (nc.sync,))
+        load_w2(3, 5)
+        load_planes(s2c, w2c_scales.rearrange(flat), (nc.sync,))
         nc.sync.dma_start(pos_t[0][:], pos1)
         nc.sync.dma_start(pos_t[1][:], pos2)
         gate_t = keep.tile([P, 2, T], F32, name="gate_t")
@@ -130,26 +119,24 @@ def tile_moe_hot_mlp_relu2_kernel(
         y3 = y[:].rearrange("p (j u) -> p j u", j=4)
         st = {}
 
-        def gather(last):
-            count = GROUPS[last]
-            e0 = last - count + 1
+        def gather(e0, count):
             n = count * C
-            base = last * REGION
-            gw = reuse.tile([P, PASSES * n], U32, name="gw%d" % last, align_bytes=64, offset=base + WORDS - PASSES * n * 4)
-            o = offs_t[:, e0 * 8:(last + 1) * 8]
-            if last == HOT - 1:
-                gp = reuse.tile([P, HOT * C], U8, name="gp", align_bytes=64, offset=base + WORDS)
+            o = offs_t[:, e0 * 8:(e0 + count) * 8]
+            gw = keep.tile([P, PASSES * n], U32, name="gw%d" % e0, align_bytes=64)
+            if e0 == 0:
+                gp = keep.tile([P, HOT * C], U8, name="gp", align_bytes=64)
                 nc.vector.tensor_copy(gp[:], xp[:].indirect(offs_t[:, 0:HOT * 8]))
                 st["gp"] = gp
-            if last >= HOT:
-                gs = reuse.tile([P, PASSES * n], U8, name="gs%d" % last, align_bytes=64, offset=base + WORDS)
+            if e0 >= HOT:
+                gs = keep.tile([P, PASSES * n], U8, name="gs%d" % e0, align_bytes=64)
             for s in range(PASSES):
                 nc.vector.tensor_copy(gw[:, s * n:(s + 1) * n], xw[:].bitcast(U32)[:, s * T:(s + 1) * T].indirect(o))
-                if last >= HOT:
-                    nc.vector.tensor_copy(gs[:, s * n:(s + 1) * n], xs[:, s * T:(s + 1) * T].indirect(o))
-            for e in range(e0, last + 1):
+                if e0 >= HOT:
+                    window = xp[:] if s == 0 else xs[:, (s - 1) * T:s * T]
+                    nc.vector.tensor_copy(gs[:, s * n:(s + 1) * n], window.indirect(o))
+            for e in range(e0, e0 + count):
                 cols = [slice(s * n + (e - e0) * C, s * n + (e - e0 + 1) * C) for s in range(PASSES)]
-                if last >= HOT:
+                if e0 >= HOT:
                     st["g", e] = [(gw[:, c], gs[:, c]) for c in cols]
                 else:
                     st["g", e] = [(gw[:, c], st["gp"][4 * s:P, e * C:(e + 1) * C]) for s, c in enumerate(cols)]
@@ -158,8 +145,8 @@ def tile_moe_hot_mlp_relu2_kernel(
             a = psum.tile([P, H], F32, name="a", bufs=2)
             hot = e < HOT
             width = H * (4 if hot else 2)
-            planes = s1[e][0]
-            first = s1[e][1] * PASSES
+            planes = s1h if hot else s1c
+            first = (e if hot else e - HOT) * PASSES
             for s in range(PASSES):
                 nc.tensor.matmul_mx(
                     out=a[:],
@@ -170,7 +157,7 @@ def tile_moe_hot_mlp_relu2_kernel(
                     start=(s == 0), stop=(s == PASSES - 1),
                 )
             r = ring.tile([P, 4, P], F32, name="r")
-            if e < LATE:
+            if e in ():
                 nc.vector.tensor_scalar_max(r[:], a[:].rearrange("p (m j) -> p j m", j=4), 0.0)
             else:
                 nc.scalar.activation(r[:], a[:].rearrange("p (m j) -> p j m", j=4), ACT.Relu)
@@ -181,53 +168,60 @@ def tile_moe_hot_mlp_relu2_kernel(
             b = psum.tile([P, 4, P], F32, name="b", bufs=2)
             for j in range(4):
                 nc.tensor.transpose(b[:, j, :], r[:, j, :], ident[:])
-            if e in AFTER:
-                hb = reuse.tile([P, C, 4], BF16, name="hb%d" % e, align_bytes=64, offset=AFTER[e] * REGION + WORDS - 512)
-            else:
-                hb = ring.tile([P, C, 4], BF16, name="hb", align_bytes=64)
+            hb = ring.tile([P, C, 4], BF16, name="hb", align_bytes=64)
             nc.scalar.activation(hb[:], b[:].rearrange("p j u -> p u j"), ACT.Square)
             hq = ring.tile([P, C], U32, name="hq", align_bytes=64)
             hs = ring.tile([P, C], U8, name="hs", align_bytes=64)
             nc.vector.quantize_mx(out=hq[:].bitcast(FP8X4), scales=hs[:], in_=hb[:].rearrange("p u j -> p (u j)"))
             st["q", e] = (hq, hs)
 
-        def layer2(e):
-            hq, hs = st["q", e]
+        def deal(e):
             hot = e < HOT
+            size = 4 if hot else 2
+            dw = keep.tile([P, N * size], U8, name="dw%d" % e, align_bytes=64)
+            ds = keep.tile([P, N], U8, name="ds%d" % e, align_bytes=64)
+            dt = U32 if hot else U16
+            run = 16 // size
+            src = w2[e].bitcast(dt).rearrange("p (c i j) -> p c j i", i=run, j=4)
+            dst = dw[:].bitcast(dt).rearrange("p (j c i) -> p c j i", i=run, j=4)
+            if e in range(8):
+                nc.vector.tensor_copy(dst, src)
+            else:
+                nc.scalar.copy(dst, src)
             planes = s2h if hot else s2c
             first = e if hot else e - HOT
-            c = psum.tile([P, N], F32, name="c", bufs=2)
-            nc.tensor.matmul_mx(
-                out=c[:],
-                lhsT=hq[:].bitcast(FP8X4),
-                lhsT_scale=hs[:],
-                rhs=w2[e].bitcast(FP8X4 if hot else FP4X4),
-                rhs_scale=planes[:, first * N:(first + 1) * N],
-                start=True, stop=True,
+            nc.vector.tensor_copy(
+                ds[:].rearrange("p (j c i) -> p c j i", i=16, j=4),
+                planes[:, first * N:(first + 1) * N].rearrange("p (c i j) -> p c j i", i=16, j=4),
             )
-            yt = ring.tile([P, 4, P], F32, name="yt")
-            if e < LATE:
-                nc.vector.tensor_copy(yt[:], c[:].rearrange("p (m j) -> p j m", j=4))
-            else:
-                nc.scalar.copy(yt[:], c[:].rearrange("p (m j) -> p j m", j=4))
-            st["yt", e] = yt
+            st["d", e] = (dw, ds)
 
-        def turn2(e):
-            yt = st["yt", e]
-            d = psum.tile([P, 4, P], F32, name="d", bufs=2)
+        def layer2(e):
+            hq, hs = st["q", e]
+            dw, ds = st["d", e]
+            hot = e < HOT
+            width = P * (4 if hot else 2)
+            c = psum.tile([P, 4, C], F32, name="c", bufs=4)
             for j in range(4):
-                nc.tensor.transpose(d[:, j, :], yt[:, j, :], ident[:])
-            nc.scalar.copy(y3[:, :, e * C:(e + 1) * C], d[:])
+                nc.tensor.matmul_mx(
+                    out=c[:, j, :],
+                    lhsT=dw[:, j * width:(j + 1) * width].bitcast(FP8X4 if hot else FP4X4),
+                    lhsT_scale=ds[:, j * P:(j + 1) * P],
+                    rhs=hq[:].bitcast(FP8X4),
+                    rhs_scale=hs[:],
+                    start=True, stop=True,
+                )
+            if e in (7,):
+                nc.vector.tensor_copy(y3[:, :, e * C:(e + 1) * C], c[:])
+            else:
+                nc.scalar.copy(y3[:, :, e * C:(e + 1) * C], c[:])
 
-        gather(7)
-        gather(6)
-        for step in range(1, E + 4):
-            for back, stage in ((4, turn2), (2, turn1), (3, layer2), (1, layer1)):
+        for e0, count in GROUPS:
+            gather(e0, count)
+        for step in range(1, E + 9):
+            for back, stage in ((1, layer1), (2, turn1), (7, deal), (8, layer2)):
                 if 0 <= step - back < E:
-                    e = ORDER[step - back]
-                    stage(e)
-                    if stage is turn1 and e in AFTER:
-                        gather(AFTER[e])
+                    stage(step - back)
 
         codes = keep.tile([P, T], I32, name="codes", align_bytes=64)
         oscale = keep.tile([P, T], U8, name="oscale", align_bytes=64)

from contextlib import ExitStack

import concourse.mybir as mybir
from concourse.masks import make_identity

K, T, E, C, H, N, HOT = 1536, 512, 8, 128, 512, 512, 3
COLD = E - HOT
FLOPS = 2 * E * C * (K * H + H * N)

F32 = mybir.dt.float32
BF16 = mybir.dt.bfloat16
I32 = mybir.dt.int32
U32 = mybir.dt.uint32
U16 = mybir.dt.uint16
U8 = mybir.dt.uint8
FP8X4 = mybir.dt.float8_e4m3fn_x4
FP4X4 = mybir.dt.float4_e2m1fn_x4
ACT = mybir.ActivationFunctionType
ALU = mybir.AluOpType

P = 128
PASSES = K // 512
SLOTS = E * C
GROUPS = ((0, 1), (1, 2), (3, 2), (5, 2), (7, 1))
CHUNKS = ((0, 384), (384, 128))


def tile_moe_hot_mlp_relu2_kernel(
    tc, x_words, x_scales, w1h_words, w1h_scales, w2h_words, w2h_scales,
    w1c_words, w1c_scales, w2c_words, w2c_scales, gate, offs, pos1, pos2, out_0, out_1, out_2,
):
    nc = tc.nc
    with ExitStack() as ctx:
        lists = ctx.enter_context(tc.tile_pool(name="lists", bufs=1))
        keep = ctx.enter_context(tc.tile_pool(name="keep", bufs=1))
        ring = ctx.enter_context(tc.tile_pool(name="ring", bufs=8))
        psum = ctx.enter_context(tc.psum_pool(name="psum", bufs=1))

        def plane_tile(name, planes, engine):
            t = keep.tile([P, planes * 512], U8, name=name, align_bytes=64)
            engine.memset(t[:].bitcast(I32), 0)
            return t

        def load_planes(t, src, queues=(nc.sync,)):
            rows = src.bitcast(I32)
            view = t[:].bitcast(I32).rearrange("p (g n) -> p g n", n=128)
            for r in range(4):
                queues[r % len(queues)].dma_start(out=view[r:P:32], in_=rows[:, r:16:4, :].rearrange("g q n -> q g n"))

        xp = plane_tile("xp", 1, nc.gpsimd)
        s1h = plane_tile("s1h", HOT * PASSES, nc.gpsimd)
        s1c = plane_tile("s1c", COLD * PASSES, nc.vector)
        xs = plane_tile("xs", PASSES - 1, nc.vector)
        s2h = plane_tile("s2h", HOT, nc.vector)
        s2c = plane_tile("s2c", COLD, nc.vector)
        ident = keep.tile([P, P], F32, name="ident")

        offs_t = lists.tile([P, SLOTS // 16], U16, name="offs_t")
        pos_t = [lists.tile([P, T // 16], U16, name="pos%d_t" % r) for r in (1, 2)]
        xw = keep.tile([P, PASSES * T], I32, name="xw", align_bytes=64)
        w1 = {}
        w2 = {}

        def load_w1(first, count):
            if first < HOT:
                width = PASSES * H * 4
                src = w1h_words[first:first + count].rearrange("e s p i d -> p (e s) (i d)").bitcast(I32)
            else:
                width = PASSES * H * 2
                src = w1c_words[first - HOT:first - HOT + count].bitcast(I32).rearrange("e s p w -> p (e s) w")
            t = keep.tile([P, count * width], U8, name="w1_%d" % first, align_bytes=64)
            nc.sync.dma_start(out=t[:].bitcast(I32).rearrange("p (g w) -> p g w", g=count * PASSES), in_=src)
            for i in range(count):
                w1[first + i] = t[:, i * width:(i + 1) * width]

        def load_w2(first, count):
            if first < HOT:
                width = N * 4
                src = w2h_words[first:first + count, 0].rearrange("e p n d -> p e (n d)").bitcast(I32)
            else:
                width = N * 2
                src = w2c_words[first - HOT:first - HOT + count, 0].bitcast(I32).rearrange("e p w -> p e w")
            t = keep.tile([P, count * width], U8, name="w2_%d" % first, align_bytes=64)
            nc.sync.dma_start(out=t[:].bitcast(I32).rearrange("p (e w) -> p e w", e=count), in_=src)
            for i in range(count):
                w2[first + i] = t[:, i * width:(i + 1) * width]

        flat = "e s b i -> (e s) b i"
        make_identity(nc, ident[:])
        nc.sync.dma_start(offs_t[:], offs)
        nc.sync.dma_start(
            out=xw[:].rearrange("p (s t) -> p s t", s=PASSES),
            in_=x_words.rearrange("s p t d -> p s (t d)").bitcast(I32),
        )
        for q in range(4):
            (nc.scalar,)[q % 1].dma_start(
                out=xp[:].bitcast(I32)[32 * q:32 * q + 4 * PASSES, :],
                in_=x_scales.bitcast(I32)[:, 4 * q:4 * q + 4, :],
            )
        load_w1(0, 1)
        load_planes(s1h, w1h_scales.rearrange(flat), (nc.scalar, nc.sync,))
        load_planes(xs, x_scales[1:PASSES], (nc.sync,))
        load_planes(s1c, w1c_scales.rearrange(flat), (nc.scalar,))
        load_w1(1, 1)
        load_w1(2, 1)
        load_w1(3, 2)
        load_w1(5, 2)
        load_w1(7, 1)
        load_w2(0, 3)
        load_planes(s2h, w2h_scales.rearrange(flat), (nc.sync,))
        load_w2(3, 5)
        load_planes(s2c, w2c_scales.rearrange(flat), (nc.sync,))
        nc.sync.dma_start(pos_t[0][:], pos1)
        nc.sync.dma_start(pos_t[1][:], pos2)
        gate_t = keep.tile([P, 2, T], F32, name="gate_t")
        nc.sync.dma_start(out=gate_t[:], in_=gate.rearrange("r p t -> p r t"))

        y = keep.tile([P, 4 * SLOTS], F32, name="y")
        y3 = y[:].rearrange("p (j u) -> p j u", j=4)
        st = {}

        def gather(e0, count):
            n = count * C
            o = offs_t[:, e0 * 8:(e0 + count) * 8]
            gw = keep.tile([P, PASSES * n], U32, name="gw%d" % e0, align_bytes=64)
            if e0 == 0:
                gp = keep.tile([P, HOT * C], U8, name="gp", align_bytes=64)
                nc.vector.tensor_copy(gp[:], xp[:].indirect(offs_t[:, 0:HOT * 8]))
                st["gp"] = gp
            if e0 >= HOT:
                gs = keep.tile([P, PASSES * n], U8, name="gs%d" % e0, align_bytes=64)
            for s in range(PASSES):
                nc.vector.tensor_copy(gw[:, s * n:(s + 1) * n], xw[:].bitcast(U32)[:, s * T:(s + 1) * T].indirect(o))
                if e0 >= HOT:
                    window = xp[:] if s == 0 else xs[:, (s - 1) * T:s * T]
                    nc.vector.tensor_copy(gs[:, s * n:(s + 1) * n], window.indirect(o))
            for e in range(e0, e0 + count):
                cols = [slice(s * n + (e - e0) * C, s * n + (e - e0 + 1) * C) for s in range(PASSES)]
                if e0 >= HOT:
                    st["g", e] = [(gw[:, c], gs[:, c]) for c in cols]
                else:
                    st["g", e] = [(gw[:, c], st["gp"][4 * s:P, e * C:(e + 1) * C]) for s, c in enumerate(cols)]

        def layer1(e):
            a = psum.tile([P, H], F32, name="a", bufs=2)
            hot = e < HOT
            width = H * (4 if hot else 2)
            planes = s1h if hot else s1c
            first = (e if hot else e - HOT) * PASSES
            for s in range(PASSES):
                nc.tensor.matmul_mx(
                    out=a[:],
                    lhsT=st["g", e][s][0].bitcast(FP8X4),
                    lhsT_scale=st["g", e][s][1],
                    rhs=w1[e][:, s * width:(s + 1) * width].bitcast(FP8X4 if hot else FP4X4),
                    rhs_scale=planes[:, (first + s) * H:(first + s + 1) * H],
                    start=(s == 0), stop=(s == PASSES - 1),
                )
            r = ring.tile([P, 4, P], F32, name="r")
            if e in ():
                nc.vector.tensor_scalar_max(r[:], a[:].rearrange("p (m j) -> p j m", j=4), 0.0)
            else:
                nc.scalar.activation(r[:], a[:].rearrange("p (m j) -> p j m", j=4), ACT.Relu)
            st["r", e] = r

        def turn1(e):
            r = st["r", e]
            b = psum.tile([P, 4, P], F32, name="b", bufs=2)
            for j in range(4):
                nc.tensor.transpose(b[:, j, :], r[:, j, :], ident[:])
            hb = ring.tile([P, C, 4], BF16, name="hb", align_bytes=64)
            nc.scalar.activation(hb[:], b[:].rearrange("p j u -> p u j"), ACT.Square)
            hq = ring.tile([P, C], U32, name="hq", align_bytes=64)
            hs = ring.tile([P, C], U8, name="hs", align_bytes=64)
            nc.vector.quantize_mx(out=hq[:].bitcast(FP8X4), scales=hs[:], in_=hb[:].rearrange("p u j -> p (u j)"))
            st["q", e] = (hq, hs)

        def deal(e):
            hot = e < HOT
            size = 4 if hot else 2
            dw = keep.tile([P, N * size], U8, name="dw%d" % e, align_bytes=64)
            ds = keep.tile([P, N], U8, name="ds%d" % e, align_bytes=64)
            dt = U32 if hot else U16
            run = 16 // size
            src = w2[e].bitcast(dt).rearrange("p (c i j) -> p c j i", i=run, j=4)
            dst = dw[:].bitcast(dt).rearrange("p (j c i) -> p c j i", i=run, j=4)
            if e in range(8):
                nc.vector.tensor_copy(dst, src)
            else:
                nc.scalar.copy(dst, src)
            planes = s2h if hot else s2c
            first = e if hot else e - HOT
            nc.vector.tensor_copy(
                ds[:].rearrange("p (j c i) -> p c j i", i=16, j=4),
                planes[:, first * N:(first + 1) * N].rearrange("p (c i j) -> p c j i", i=16, j=4),
            )
            st["d", e] = (dw, ds)

        def layer2(e):
            hq, hs = st["q", e]
            dw, ds = st["d", e]
            hot = e < HOT
            width = P * (4 if hot else 2)
            c = psum.tile([P, 4, C], F32, name="c", bufs=4)
            for j in range(4):
                nc.tensor.matmul_mx(
                    out=c[:, j, :],
                    lhsT=dw[:, j * width:(j + 1) * width].bitcast(FP8X4 if hot else FP4X4),
                    lhsT_scale=ds[:, j * P:(j + 1) * P],
                    rhs=hq[:].bitcast(FP8X4),
                    rhs_scale=hs[:],
                    start=True, stop=True,
                )
            if e in (7,):
                nc.vector.tensor_copy(y3[:, :, e * C:(e + 1) * C], c[:])
            else:
                nc.scalar.copy(y3[:, :, e * C:(e + 1) * C], c[:])

        for e0, count in GROUPS:
            gather(e0, count)
        for step in range(1, E + 9):
            for back, stage in ((1, layer1), (2, turn1), (7, deal), (8, layer2)):
                if 0 <= step - back < E:
                    stage(step - back)

        codes = keep.tile([P, T], I32, name="codes", align_bytes=64)
        oscale = keep.tile([P, T], U8, name="oscale", align_bytes=64)
        out_rows = out_0.rearrange("(p j) t -> p j t", j=4)
        out_words = out_1[0].rearrange("p t d -> p (t d)").bitcast(I32)
        for n, (t0, w) in enumerate(CHUNKS):
            g = [keep.tile([P, 4, w], F32, name="g%d_%d" % (r, n)) for r in range(2)]
            o = keep.tile([P, 4, w], F32, name="o_%d" % n)
            step = 1 if n == 0 else 2
            for j0 in range(0, 4, step):
                j1 = j0 + step
                for r in range(2):
                    for j in range(j0, j1):
                        src = y[:, j * SLOTS:(j + 1) * SLOTS].indirect(pos_t[r][:, t0 // 16:(t0 + w) // 16])
                        if n == 0 and r == 0 and j < 2:
                            nc.vector.tensor_copy(g[r][:, j, :], src)
                        else:
                            nc.scalar.activation(g[r][:, j, :], src, ACT.Copy)
                for r in range(2):
                    nc.vector.tensor_tensor(
                        g[r][:, j0:j1, :], g[r][:, j0:j1, :],
                        gate_t[:, r:r + 1, t0:t0 + w].to_broadcast([P, j1 - j0, w]), ALU.mult,
                    )
                nc.vector.tensor_tensor(o[:, j0:j1, :], g[0][:, j0:j1, :], g[1][:, j0:j1, :], ALU.add)
            nc.sync.dma_start(out=out_rows[:, :, t0:t0 + w], in_=o[:])
            ob = keep.tile([P, w, 4], BF16, name="ob_%d" % n, align_bytes=64)
            if n == 0:
                nc.scalar.copy(ob[:], o[:].rearrange("p j t -> p t j"))
            else:
                nc.vector.tensor_copy(ob[:], o[:].rearrange("p j t -> p t j"))
            nc.vector.quantize_mx(
                out=codes[:, t0:t0 + w].bitcast(FP8X4), scales=oscale[:, t0:t0 + w],
                in_=ob[:].rearrange("p t j -> p (t j)"),
            )
            nc.sync.dma_start(out=out_words[:, t0:t0 + w], in_=codes[:, t0:t0 + w])
        for r in range(4):
            queue = nc.sync if r % 2 == 0 else nc.scalar
            queue.dma_start(out=out_2[0].bitcast(I32)[r:16:4, :], in_=oscale[:].bitcast(I32)[r:P:32, :])
